import numpy as np
import ml_dtypes


def mxq(x, axis, fmt="e4m3"):
    dtype, down = {"e4m3": (ml_dtypes.float8_e4m3fn, 7), "e5m2": (ml_dtypes.float8_e5m2, 14)}[fmt]
    v = np.moveaxis(np.asarray(x, np.float32).astype(ml_dtypes.bfloat16).astype(np.float64), axis, -1)
    blocks = v.reshape(v.shape[:-1] + (-1, 32))
    amax = np.abs(blocks).max(-1, keepdims=True)
    byte = np.maximum(np.where(amax > 0, np.frexp(amax)[1] - 1 + 127, 0) - down, 1)
    scale = np.exp2(byte - 127.0)
    codes = (blocks / scale).astype(np.float32).astype(dtype).astype(np.float64)
    return np.moveaxis((codes * scale).reshape(v.shape), -1, axis)


WIDE = False


def mx_kscale(k):
    if not WIDE:
        return np.ones(k)
    levels = np.array([10, -10, 5, -5, 0])
    if k % 512:
        return np.exp2(np.random.permutation(np.resize(levels, k // 32))).repeat(32)
    a = np.empty((k // 512, 16))
    for p in range(k // 512):
        a[p, :8] = np.random.permutation(np.resize(levels, 8))
        for g in range(8):
            far = levels[np.abs(levels - a[p, g]) >= 10]
            a[p, g + 8] = far[np.random.randint(len(far))]
    return np.exp2(a.ravel()).repeat(32)


def f64(x):
    return np.asarray(x).astype(np.float64)


def striped(idx):
    return np.tile(idx.reshape(-1, 16).T, (8, 1)).astype(np.uint16)


def unstriped(offs):
    return offs[:16].T.reshape(-1).astype(np.int64)


def pack_weight(w):
    k, n = w.shape
    w = f64(np.asarray(w, np.float32).astype(ml_dtypes.bfloat16)).reshape(k // 32, 32, n)
    amax = np.abs(w).max(1)
    byte = np.clip(np.where(amax > 0, np.frexp(amax)[1] - 1 + 127 - 7, 1), 1, 254)
    scaled = (w * np.exp2(127.0 - byte)[:, None, :]).reshape(k, n).astype(np.float32)
    words = np.ascontiguousarray(scaled.reshape(k // 512, 128, 4, n).transpose(0, 1, 3, 2)).astype(ml_dtypes.float8_e4m3fn).view(np.uint8)
    return words, np.ascontiguousarray(byte.astype(np.uint8).reshape(k // 512, 16, n))


def unpack_weight(words, scales):
    g, p, n, _ = words.shape
    vals = np.ascontiguousarray(words).view(ml_dtypes.float8_e4m3fn).astype(np.float64) * np.repeat(np.exp2(scales.astype(np.float64) - 127.0), 8, axis=1)[..., None]
    return vals.transpose(0, 1, 3, 2).reshape(g * 512, n)


K, T, S, N, H = 1024, 2048, 512, 128, 512


def setup_inputs():
    n = np.random.standard_normal
    s = mx_kscale(K)[:, None]
    u = mx_kscale(H)
    packed_xT = pack_weight(n((K, T)) * s)
    return {
        "x_words": packed_xT[0],
        "x_scales": packed_xT[1],
        "w1": (n((K, H)) / np.sqrt(K) / s).astype(np.float32),
        "w2": (n((K, H)) / np.sqrt(K) / s).astype(np.float32),
        "intf": (np.random.uniform(0.2, 0.8, (H, S))).astype(np.float32),
        "age": (np.random.uniform(0.3, 2.5, (H, S))).astype(np.float32),
        "unit": (np.random.uniform(0.6, 1.4, (H, 1)) * u[:, None]).astype(np.float32),
        "w3": (n((H, N)) / np.sqrt(H) / u[:, None]).astype(np.float32),
        "offs": striped(np.random.permutation(T)[:S]),
        "off": striped(np.random.permutation(S)),
    }


def reference(x_words, x_scales, w1, w2, intf, age, unit, w3, offs, off):
    xq = unpack_weight(x_words, x_scales)[:, unstriped(offs)]
    qi = mxq(f64(w2), 0, "e4m3").T @ xq
    init = np.exp(0.9 * np.tanh(qi))
    di = mxq(f64(w1), 0, "e4m3").T @ xq
    dec = 0.5 * (np.log(np.exp(di) + 1.0)) + 0.1
    do = dec[:, unstriped(off)]
    itf = do * f64(intf)
    den = 0.6 * ((dec + itf) * f64(age)) + 1.0
    rate = init / ((den) ** 2)
    ro = rate[:, unstriped(off)]
    hid = f64(unit) * (rate - (0.4 * ro))
    return mxq(f64(w3), 0, "e4m3").T @ mxq(hid, 0, "e4m3")

@@ -1,0 +1,259 @@
+import math
+from contextlib import ExitStack
+
+import concourse.mybir as mybir
+
+K, T, S, N, H = 1024, 2048, 512, 128, 512
+FLOPS = 2 * (2 * K * H * S + H * N * S)
+
+F32 = mybir.dt.float32
+BF16 = mybir.dt.bfloat16
+I32 = mybir.dt.int32
+U32 = mybir.dt.uint32
+U16 = mybir.dt.uint16
+U8 = mybir.dt.uint8
+FP8X4 = mybir.dt.float8_e4m3fn_x4
+ALU = mybir.AluOpType
+ACT = mybir.ActivationFunctionType
+
+P = 128
+PACK = 4
+K_PASS = P * PACK
+PASSES = K // K_PASS
+SPARE = 16
+HALF = S // 2
+EXP_CAP = 30.0
+
+
+def tile_picked_yarpsd_hyp_p_kernel(
+    tc, x_words, x_scales, w1, w2, intf, age, unit, w3, offs, off, out
+):
+    nc = tc.nc
+    with ExitStack() as ctx:
+        keep = ctx.enter_context(tc.tile_pool(name="keep", bufs=1))
+        psum = ctx.enter_context(tc.psum_pool(name="psum", bufs=1))
+
+        def sb(name, shape, dtype, tag=None):
+            return keep.tile(shape, dtype, name=name, tag=tag or name, align_bytes=64)
+
+        x_table = [sb("x_table%d" % o, [P, T], U32) for o in range(PASSES)]
+        scale_table = sb("scale_table", [P, T], U8)
+        picks = keep.tile([P, S // 16], U16, name="picks")
+        offsets = keep.tile([P, S // 16], U16, name="offsets")
+        nc.vector.memset(scale_table[:].bitcast(I32), 0)
+
+        def load_x(o):
+            nc.sync.dma_start(
+                out=x_table[o][:].bitcast(I32),
+                in_=x_words[o].rearrange("p n t -> p (n t)").bitcast(I32),
+            )
+
+        def load_rows(name, src, o):
+            raw = sb(name, [P, PACK, src.shape[1]], F32)
+            nc.sync.dma_start(
+                out=raw[:], in_=src[o * K_PASS : (o + 1) * K_PASS, :].rearrange("(p j) c -> p j c", j=PACK)
+            )
+            return raw
+
+        load_x(0)
+        nc.sync.dma_start(out=picks[:], in_=offs)
+        for q in range(4):
+            nc.sync.dma_start(
+                out=scale_table[32 * q : 32 * q + 4 * PASSES, :].bitcast(I32),
+                in_=x_scales[:, 4 * q : 4 * q + 4, :].bitcast(I32),
+            )
+        w1_raw = [load_rows("w1_raw0", w1, 0)]
+        load_x(1)
+        w1_last = []
+        for h in range(2):
+            part = sb("w1_last%d" % h, [P, PACK, H // 2], F32)
+            nc.sync.dma_start(
+                out=part[:],
+                in_=w1[K_PASS:, h * H // 2 : (h + 1) * H // 2].rearrange("(p j) c -> p j c", j=PACK),
+            )
+            w1_last.append(part)
+        w2_raw = [load_rows("w2_raw0", w2, 0)]
+        w3_raw = load_rows("w3_raw", w3, 0)
+        nc.sync.dma_start(out=offsets[:], in_=off)
+        unit_sb = sb("unit_sb", [P, PACK], F32)
+        nc.sync.dma_start(out=unit_sb[:], in_=unit.rearrange("(p t) o -> p (t o)", t=PACK))
+        intf_sb = load_rows("intf_sb", intf, 0)
+        age_sb = load_rows("age_sb", age, 0)
+        w2_raw.append(load_rows("w2_raw1", w2, 1))
+
+        one = sb("one", [P, 1], F32)
+        shift = sb("shift", [P, 1], F32)
+        nc.vector.memset(one[:], 1.0)
+        nc.vector.tensor_scalar(shift[:], one[:], math.exp(0.2), None, ALU.mult)
+        dec2 = [sb("dec2_%d" % t, [P, S + SPARE], F32) for t in range(PACK)]
+        taken = [sb("taken%d" % t, [P, S + SPARE], F32) for t in range(PACK)]
+        for t in range(PACK):
+            nc.vector.memset(dec2[t][:, S:], 0.0)
+            nc.vector.memset(taken[t][:, S:], 0.0)
+
+        x_codes = [sb("x_codes%d" % o, [P, S], U32) for o in range(PASSES)]
+        x_bytes = sb("x_bytes", [P, S], U8)
+        nc.vector.tensor_copy(x_codes[0][:], x_table[0][:].indirect(picks[:]))
+        nc.vector.tensor_copy(x_bytes[:], scale_table[:].indirect(picks[:]))
+
+        def cast(engine, dst, src):
+            if engine == "scalar":
+                nc.scalar.activation(out=dst, in_=src, func=ACT.Copy)
+            else:
+                nc.vector.tensor_copy(out=dst, in_=src)
+
+        def deal_into(grouped, raw, t0, count, m0, engine):
+            src = raw[:].rearrange("p j (m t) -> p m j t", t=PACK)[:, :, :, t0 : t0 + count]
+            cast(engine, grouped.rearrange("p t m j -> p m j t")[:, m0 : m0 + src.shape[1]], src)
+
+        def deal(name, raw, t0, count, engine):
+            grouped = sb(name, [P, count, P, PACK], BF16)
+            deal_into(grouped[:], raw, t0, count, 0, engine)
+            return grouped[:]
+
+        def quantize(name, flat, words):
+            codes = sb(name + "_codes", [P, words], U32)
+            scales = sb(name + "_scales", [P, words], U8)
+            nc.vector.quantize_mx(out=codes[:].bitcast(FP8X4), scales=scales[:], in_=flat)
+            return codes, scales
+
+        def quantize_dealt(name, grouped, count):
+            codes, scales = quantize(name, grouped.rearrange("p t m j -> p (t m j)"), count * P)
+            return [(codes[:, i * P : (i + 1) * P], scales[:, i * P : (i + 1) * P]) for i in range(count)]
+
+        def first_product(banks, weights, o):
+            for t in range(PACK):
+                nc.tensor.matmul_mx(
+                    out=banks[t][:],
+                    lhsT=weights[t][0].bitcast(FP8X4),
+                    lhsT_scale=weights[t][1],
+                    rhs=x_codes[o][:].bitcast(FP8X4),
+                    rhs_scale=x_bytes[4 * o :, :],
+                    start=(o == 0),
+                    stop=(o == PASSES - 1),
+                )
+
+        di = [psum.tile([P, S], F32, name="di%d" % t) for t in range(PACK)]
+        qi = [psum.tile([P, S], F32, name="qi%d" % t) for t in range(PACK)]
+
+        low = deal("w1g0a", w1_raw[0], 0, 2, "vector")
+        high = deal("w1g0b", w1_raw[0], 2, 2, "scalar")
+        first_product(di, quantize_dealt("w1p0a", low, 2) + quantize_dealt("w1p0b", high, 2), 0)
+        nc.vector.tensor_copy(x_codes[1][:], x_table[1][:].indirect(picks[:]))
+        low = sb("w1g1a", [P, 2, P, PACK], BF16)
+        high = sb("w1g1b", [P, 2, P, PACK], BF16)
+        for h in range(2):
+            deal_into(low[:], w1_last[h], 0, 2, h * P // 2, "vector")
+            deal_into(high[:], w1_last[h], 2, 2, h * P // 2, "scalar")
+        first_product(di, quantize_dealt("w1p1a", low[:], 2) + quantize_dealt("w1p1b", high[:], 2), 1)
+
+        capped = sb("capped", [P, PACK, S], F32, tag="before_ln")
+        grown = sb("grown", [P, PACK, S], F32)
+        for t in range(PACK):
+            nc.vector.tensor_scalar(capped[:, t, :], di[t][:], EXP_CAP, None, ALU.min)
+            nc.scalar.activation(out=grown[:, t, :], in_=capped[:, t, :], func=ACT.Exp)
+
+        first_product(qi, quantize_dealt("w2p0", deal("w2g0", w2_raw[0], 0, 4, "vector"), 4), 0)
+
+        w3_grouped = sb("w3_grouped", [P, N, PACK], BF16)
+        nc.vector.tensor_copy(
+            out=w3_grouped[:].rearrange("p (c i) j -> p c j i", i=4),
+            in_=w3_raw[:].rearrange("p j (c i) -> p c j i", i=4),
+        )
+        w3_codes, w3_scales = quantize("w3", w3_grouped[:].rearrange("p c j -> p (c j)"), N)
+        unit_off = sb("unit_off", [P, PACK], F32)
+        nc.vector.tensor_scalar(unit_off[:], unit_sb[:], -0.4, None, ALU.mult)
+
+        soft = sb("soft", [P, PACK, S], F32, tag="before_ln")
+        for t in range(PACK):
+            nc.scalar.activation(
+                out=soft[:, t, :], in_=grown[:, t, :], func=ACT.Ln, scale=math.exp(0.2), bias=shift[:]
+            )
+
+        squared = sb("squared", [P, PACK, S], F32, tag="before_tanh")
+        log_den = sb("log_den", [P, PACK, S], F32)
+        itf = [sb("itf%d" % t, [P, S], F32) for t in range(PACK)]
+        fetched = [sb("fetched%d" % t, [P, S], F32) for t in range(1, PACK)]
+        for t in range(PACK):
+            nc.vector.scalar_tensor_tensor(
+                out=dec2[t][:, :S], in0=di[t][:], scalar=0.2, in1=soft[:, t, :], op0=ALU.add, op1=ALU.max
+            )
+            if t == 1:
+                nc.vector.tensor_tensor(itf[0][:], dec2[0][:].indirect(offsets[:]), intf_sb[:, 0, :], ALU.mult)
+            if t > 0:
+                nc.scalar.activation(out=fetched[t - 1][:], in_=dec2[t][:].indirect(offsets[:]), func=ACT.Copy)
+        for t in range(PACK):
+            if t > 0:
+                nc.vector.tensor_tensor(itf[t][:], fetched[t - 1][:], intf_sb[:, t, :], ALU.mult)
+            total = sb("total%d" % t, [P, S], F32)
+            nc.vector.tensor_tensor(total[:], itf[t][:], dec2[t][:, :S], ALU.add)
+            aged = sb("aged%d" % t, [P, S], F32)
+            nc.vector.tensor_tensor(aged[:], total[:], age_sb[:, t, :], ALU.mult)
+            nc.scalar.activation(out=squared[:, t, :], in_=aged[:], func=ACT.Square, scale=0.3, bias=one[:])
+            nc.scalar.activation(out=log_den[:, t, :], in_=squared[:, t, :], func=ACT.Ln)
+
+        w2_last = sb("w2_last", [P, 2, 2, P, PACK], BF16, tag="age_sb")
+        for h in range(2):
+            deal_into(w2_last[:, h], w2_raw[1], 2 * h, 2, 0, "vector")
+        first_product(qi, quantize_dealt("w2p1a", w2_last[:, 0], 2) + quantize_dealt("w2p1b", w2_last[:, 1], 2), 1)
+
+        bent = sb("bent", [P, PACK, S], F32, tag="before_tanh")
+        hid = sb("hid", [P, PACK, S], F32)
+        log_rate = [sb("log_rate%d" % t, [P, S], F32) for t in range(PACK)]
+
+        def log_of_rate(t):
+            nc.scalar.activation(out=bent[:, t, :], in_=qi[t][:], func=ACT.Tanh)
+            nc.vector.scalar_tensor_tensor(
+                out=log_rate[t][:], in0=bent[:, t, :], scalar=0.9, in1=log_den[:, t, :], op0=ALU.mult, op1=ALU.subtract
+            )
+
+        def hidden(t):
+            rate = sb("rate%d" % t, [P, S], F32)
+            nc.scalar.activation(out=rate[:], in_=log_rate[t][:], func=ACT.Exp)
+            if t < PACK - 1:
+                nc.vector.tensor_scalar(taken[t][:, :S], rate[:], unit_off[:, t : t + 1], None, ALU.mult)
+            else:
+                nc.scalar.activation(out=taken[t][:, :S], in_=rate[:], func=ACT.Copy, scale=unit_off[:, t : t + 1])
+            own = sb("own%d" % t, [P, S], F32)
+            nc.scalar.activation(out=own[:], in_=rate[:], func=ACT.Copy, scale=unit_sb[:, t : t + 1])
+            if t < PACK - 1:
+                nc.vector.tensor_tensor(hid[:, t, :], taken[t][:].indirect(offsets[:]), own[:], ALU.add)
+            else:
+                for h in range(2):
+                    cols = slice(h * HALF, (h + 1) * HALF)
+                    nc.vector.tensor_tensor(
+                        hid[:, t, cols],
+                        taken[t][:].indirect(offsets[:, h * HALF // 16 : (h + 1) * HALF // 16]),
+                        own[:, cols],
+                        ALU.add,
+                    )
+
+        for t in range(PACK):
+            log_of_rate(t)
+        for t in range(PACK):
+            hidden(t)
+
+        hid_grouped = []
+        for h, engine in enumerate(("scalar", "vector")):
+            grouped = sb("hid_grouped%d" % h, [P, HALF, PACK], BF16)
+            cast(
+                engine,
+                grouped[:].rearrange("p (c i) t -> p c t i", i=4),
+                hid[:, :, h * HALF : (h + 1) * HALF].rearrange("p t (c i) -> p c t i", i=4),
+            )
+            hid_grouped.append(grouped)
+        for h in (1, 0):
+            codes, scales = quantize("hid%d" % h, hid_grouped[h][:].rearrange("p c t -> p (c t)"), HALF)
+            acc = psum.tile([P, HALF], F32, name="acc%d" % h, tag="di%d" % h)
+            nc.tensor.matmul_mx(
+                out=acc[:],
+                lhsT=w3_codes[:].bitcast(FP8X4),
+                lhsT_scale=w3_scales[:],
+                rhs=codes[:].bitcast(FP8X4),
+                rhs_scale=scales[:],
+                start=True,
+                stop=True,
+            )
+            result = sb("result%d" % h, [P, HALF], F32)
+            cast("scalar" if h else "vector", result[:], acc[:])
+            nc.sync.dma_start(out=out[:, h * HALF : (h + 1) * HALF], in_=result[:])

@@ -55,23 +55,16 @@ def tile_picked_yarpsd_hyp_p_kernel(
             )
             return raw
 
-        load_x(0)
-        nc.sync.dma_start(out=picks[:], in_=offs)
         for q in range(4):
             nc.sync.dma_start(
                 out=scale_table[32 * q : 32 * q + 4 * PASSES, :].bitcast(I32),
                 in_=x_scales[:, 4 * q : 4 * q + 4, :].bitcast(I32),
             )
+        load_x(0)
+        nc.sync.dma_start(out=picks[:], in_=offs)
         w1_raw = [load_rows("w1_raw0", w1, 0)]
         load_x(1)
-        w1_last = []
-        for h in range(2):
-            part = sb("w1_last%d" % h, [P, PACK, H // 2], F32)
-            nc.sync.dma_start(
-                out=part[:],
-                in_=w1[K_PASS:, h * H // 2 : (h + 1) * H // 2].rearrange("(p j) c -> p j c", j=PACK),
-            )
-            w1_last.append(part)
+        w1_raw.append(load_rows("w1_raw1", w1, 1))
         w2_raw = [load_rows("w2_raw0", w2, 0)]
         w3_raw = load_rows("w3_raw", w3, 0)
         nc.sync.dma_start(out=offsets[:], in_=off)
@@ -140,12 +133,9 @@ def tile_picked_yarpsd_hyp_p_kernel(
         high = deal("w1g0b", w1_raw[0], 2, 2, "scalar")
         first_product(di, quantize_dealt("w1p0a", low, 2) + quantize_dealt("w1p0b", high, 2), 0)
         nc.vector.tensor_copy(x_codes[1][:], x_table[1][:].indirect(picks[:]))
-        low = sb("w1g1a", [P, 2, P, PACK], BF16)
-        high = sb("w1g1b", [P, 2, P, PACK], BF16)
-        for h in range(2):
-            deal_into(low[:], w1_last[h], 0, 2, h * P // 2, "vector")
-            deal_into(high[:], w1_last[h], 2, 2, h * P // 2, "scalar")
-        first_product(di, quantize_dealt("w1p1a", low[:], 2) + quantize_dealt("w1p1b", high[:], 2), 1)
+        low = deal("w1g1a", w1_raw[1], 0, 2, "vector")
+        high = deal("w1g1b", w1_raw[1], 2, 2, "scalar")
+        first_product(di, quantize_dealt("w1p1a", low, 2) + quantize_dealt("w1p1b", high, 2), 1)
 
         capped = sb("capped", [P, PACK, S], F32, tag="before_ln")
         grown = sb("grown", [P, PACK, S], F32)
@@ -182,20 +172,26 @@ def tile_picked_yarpsd_hyp_p_kernel(
                 nc.vector.tensor_tensor(itf[0][:], dec2[0][:].indirect(offsets[:]), intf_sb[:, 0, :], ALU.mult)
             if t > 0:
                 nc.scalar.activation(out=fetched[t - 1][:], in_=dec2[t][:].indirect(offsets[:]), func=ACT.Copy)
-        for t in range(PACK):
-            if t > 0:
-                nc.vector.tensor_tensor(itf[t][:], fetched[t - 1][:], intf_sb[:, t, :], ALU.mult)
-            total = sb("total%d" % t, [P, S], F32)
-            nc.vector.tensor_tensor(total[:], itf[t][:], dec2[t][:, :S], ALU.add)
-            aged = sb("aged%d" % t, [P, S], F32)
-            nc.vector.tensor_tensor(aged[:], total[:], age_sb[:, t, :], ALU.mult)
-            nc.scalar.activation(out=squared[:, t, :], in_=aged[:], func=ACT.Square, scale=0.3, bias=one[:])
-            nc.scalar.activation(out=log_den[:, t, :], in_=squared[:, t, :], func=ACT.Ln)
+        total = [sb("total%d" % t, [P, S], F32) for t in range(PACK)]
+        aged = [sb("aged%d" % t, [P, S], F32) for t in range(PACK)]
+        for step in range(1, PACK + 2):
+            if step < PACK:
+                nc.vector.tensor_tensor(itf[step][:], fetched[step - 1][:], intf_sb[:, step, :], ALU.mult)
+            if step >= 2:
+                t = step - 2
+                nc.vector.tensor_tensor(aged[t][:], total[t][:], age_sb[:, t, :], ALU.mult)
+                nc.scalar.activation(out=squared[:, t, :], in_=aged[t][:], func=ACT.Square, scale=0.3, bias=one[:])
+                nc.scalar.activation(out=log_den[:, t, :], in_=squared[:, t, :], func=ACT.Ln)
+            if step <= PACK:
+                t = step - 1
+                nc.vector.tensor_tensor(total[t][:], itf[t][:], dec2[t][:, :S], ALU.add)
 
         w2_last = sb("w2_last", [P, 2, 2, P, PACK], BF16, tag="age_sb")
+        w2_tiles = []
         for h in range(2):
             deal_into(w2_last[:, h], w2_raw[1], 2 * h, 2, 0, "vector")
-        first_product(qi, quantize_dealt("w2p1a", w2_last[:, 0], 2) + quantize_dealt("w2p1b", w2_last[:, 1], 2), 1)
+            w2_tiles.extend(quantize_dealt("w2p1_%d" % h, w2_last[:, h], 2))
+        first_product(qi, w2_tiles, 1)
 
         bent = sb("bent", [P, PACK, S], F32, tag="before_tanh")
         hid = sb("hid", [P, PACK, S], F32)
@@ -207,31 +203,38 @@ def tile_picked_yarpsd_hyp_p_kernel(
                 out=log_rate[t][:], in0=bent[:, t, :], scalar=0.9, in1=log_den[:, t, :], op0=ALU.mult, op1=ALU.subtract
             )
 
-        def hidden(t):
-            rate = sb("rate%d" % t, [P, S], F32)
-            nc.scalar.activation(out=rate[:], in_=log_rate[t][:], func=ACT.Exp)
+        rate = [sb("rate%d" % t, [P, S], F32) for t in range(PACK)]
+        own = [sb("own%d" % t, [P, S], F32) for t in range(PACK)]
+
+        def rate_taken(t):
+            nc.scalar.activation(out=rate[t][:], in_=log_rate[t][:], func=ACT.Exp)
             if t < PACK - 1:
-                nc.vector.tensor_scalar(taken[t][:, :S], rate[:], unit_off[:, t : t + 1], None, ALU.mult)
+                nc.vector.tensor_scalar(taken[t][:, :S], rate[t][:], unit_off[:, t : t + 1], None, ALU.mult)
             else:
-                nc.scalar.activation(out=taken[t][:, :S], in_=rate[:], func=ACT.Copy, scale=unit_off[:, t : t + 1])
-            own = sb("own%d" % t, [P, S], F32)
-            nc.scalar.activation(out=own[:], in_=rate[:], func=ACT.Copy, scale=unit_sb[:, t : t + 1])
-            if t < PACK - 1:
-                nc.vector.tensor_tensor(hid[:, t, :], taken[t][:].indirect(offsets[:]), own[:], ALU.add)
-            else:
-                for h in range(2):
-                    cols = slice(h * HALF, (h + 1) * HALF)
-                    nc.vector.tensor_tensor(
-                        hid[:, t, cols],
-                        taken[t][:].indirect(offsets[:, h * HALF // 16 : (h + 1) * HALF // 16]),
-                        own[:, cols],
-                        ALU.add,
-                    )
+                nc.scalar.activation(out=taken[t][:, :S], in_=rate[t][:], func=ACT.Copy, scale=unit_off[:, t : t + 1])
+
+        def hidden(t, parts):
+            nc.scalar.activation(out=own[t][:], in_=rate[t][:], func=ACT.Copy, scale=unit_sb[:, t : t + 1])
+            width = S // parts
+            for h in range(parts):
+                cols = slice(h * width, (h + 1) * width)
+                nc.vector.tensor_tensor(
+                    hid[:, t, cols],
+                    taken[t][:].indirect(offsets[:, h * width // 16 : (h + 1) * width // 16]),
+                    own[t][:, cols],
+                    ALU.add,
+                )
 
         for t in range(PACK):
             log_of_rate(t)
-        for t in range(PACK):
-            hidden(t)
+        rate_taken(0)
+        hidden(0, 1)
+        rate_taken(1)
+        rate_taken(2)
+        hidden(1, 1)
+        hidden(2, 1)
+        rate_taken(3)
+        hidden(3, 2)
 
         hid_grouped = []
         for h, engine in enumerate(("scalar", "vector")):
@@ -242,7 +245,7 @@ def tile_picked_yarpsd_hyp_p_kernel(
                 hid[:, :, h * HALF : (h + 1) * HALF].rearrange("p t (c i) -> p c t i", i=4),
             )
             hid_grouped.append(grouped)
-        for h in (1, 0):
+        for h in range(2):
             codes, scales = quantize("hid%d" % h, hid_grouped[h][:].rearrange("p c t -> p (c t)"), HALF)
             acc = psum.tile([P, HALF], F32, name="acc%d" % h, tag="di%d" % h)
             nc.tensor.matmul_mx(
@@ -255,5 +258,5 @@ def tile_picked_yarpsd_hyp_p_kernel(
                 stop=True,
             )
             result = sb("result%d" % h, [P, HALF], F32)
-            cast("scalar" if h else "vector", result[:], acc[:])
+            cast("vector" if h else "scalar", result[:], acc[:])
             nc.sync.dma_start(out=out[:, h * HALF : (h + 1) * HALF], in_=result[:])

@@ -66,28 +66,35 @@ def tile_picked_yarpsd_hyp_p_kernel(
         load_x(1)
         w1_raw.append(load_rows("w1_raw1", w1, 1))
         w2_raw = [load_rows("w2_raw0", w2, 0)]
-        w3_raw = load_rows("w3_raw", w3, 0)
         nc.sync.dma_start(out=offsets[:], in_=off)
+        intf_rows = intf.rearrange("(p t) c -> p t c", t=PACK)
+        intf_first = sb("intf_first", [P, 1, S], F32)
+        nc.sync.dma_start(out=intf_first[:], in_=intf_rows[:, :1, :])
+        w2_raw.append(load_rows("w2_raw1", w2, 1))
+        intf_rest = sb("intf_rest", [P, PACK - 1, S], F32)
+        nc.sync.dma_start(out=intf_rest[:], in_=intf_rows[:, 1:, :])
+        age_sb = load_rows("age_sb", age, 0)
+        w3_raw = load_rows("w3_raw", w3, 0)
         unit_sb = sb("unit_sb", [P, PACK], F32)
         nc.sync.dma_start(out=unit_sb[:], in_=unit.rearrange("(p t) o -> p (t o)", t=PACK))
-        intf_sb = load_rows("intf_sb", intf, 0)
-        age_sb = load_rows("age_sb", age, 0)
-        w2_raw.append(load_rows("w2_raw1", w2, 1))
 
         one = sb("one", [P, 1], F32)
         shift = sb("shift", [P, 1], F32)
         nc.vector.memset(one[:], 1.0)
         nc.vector.tensor_scalar(shift[:], one[:], math.exp(0.2), None, ALU.mult)
         dec2 = [sb("dec2_%d" % t, [P, S + SPARE], F32) for t in range(PACK)]
-        taken = [sb("taken%d" % t, [P, S + SPARE], F32) for t in range(PACK)]
-        for t in range(PACK):
-            nc.vector.memset(dec2[t][:, S:], 0.0)
-            nc.vector.memset(taken[t][:, S:], 0.0)
+        taken = [sb("taken%d" % t, [P, S + SPARE], F32) for t in range(PACK - 1)]
+        for window in dec2 + taken:
+            nc.vector.memset(window[:, S:], 0.0)
 
         x_codes = [sb("x_codes%d" % o, [P, S], U32) for o in range(PASSES)]
         x_bytes = sb("x_bytes", [P, S], U8)
         nc.vector.tensor_copy(x_codes[0][:], x_table[0][:].indirect(picks[:]))
         nc.vector.tensor_copy(x_bytes[:], scale_table[:].indirect(picks[:]))
+
+
+        def parts(split):
+            return [slice(0, HALF), slice(HALF, S)] if split else [slice(0, S)]
 
         def cast(engine, dst, src):
             if engine == "scalar":
@@ -115,7 +122,7 @@ def tile_picked_yarpsd_hyp_p_kernel(
             return [(codes[:, i * P : (i + 1) * P], scales[:, i * P : (i + 1) * P]) for i in range(count)]
 
         def first_product(banks, weights, o):
-            for t in range(PACK):
+            for t in range(len(banks)):
                 nc.tensor.matmul_mx(
                     out=banks[t][:],
                     lhsT=weights[t][0].bitcast(FP8X4),
@@ -137,104 +144,140 @@ def tile_picked_yarpsd_hyp_p_kernel(
         high = deal("w1g1b", w1_raw[1], 2, 2, "scalar")
         first_product(di, quantize_dealt("w1p1a", low, 2) + quantize_dealt("w1p1b", high, 2), 1)
 
-        capped = sb("capped", [P, PACK, S], F32, tag="before_ln")
         grown = sb("grown", [P, PACK, S], F32)
         for t in range(PACK):
-            nc.vector.tensor_scalar(capped[:, t, :], di[t][:], EXP_CAP, None, ALU.min)
-            nc.scalar.activation(out=grown[:, t, :], in_=capped[:, t, :], func=ACT.Exp)
+            nc.scalar.activation(out=grown[:, t, :], in_=di[t][:], func=ACT.Exp)
+        capped = sb("capped", [P, PACK, S], F32)
+        nc.vector.tensor_scalar(capped[:], grown[:], math.exp(EXP_CAP), None, ALU.min)
 
         first_product(qi, quantize_dealt("w2p0", deal("w2g0", w2_raw[0], 0, 4, "vector"), 4), 0)
 
-        w3_grouped = sb("w3_grouped", [P, N, PACK], BF16)
-        nc.vector.tensor_copy(
-            out=w3_grouped[:].rearrange("p (c i) j -> p c j i", i=4),
-            in_=w3_raw[:].rearrange("p j (c i) -> p c j i", i=4),
-        )
-        w3_codes, w3_scales = quantize("w3", w3_grouped[:].rearrange("p c j -> p (c j)"), N)
-        unit_off = sb("unit_off", [P, PACK], F32)
-        nc.vector.tensor_scalar(unit_off[:], unit_sb[:], -0.4, None, ALU.mult)
+        w2_early = sb("w2_early", [P, 2, P, PACK], BF16, tag="grown")
+        deal_into(w2_early[:], w2_raw[1], 0, 2, 0, "vector")
+        first_product(qi[:2], quantize_dealt("w2p1a", w2_early[:], 2), 1)
 
-        soft = sb("soft", [P, PACK, S], F32, tag="before_ln")
+        soft = sb("soft", [P, PACK, S], F32)
         for t in range(PACK):
-            nc.scalar.activation(
-                out=soft[:, t, :], in_=grown[:, t, :], func=ACT.Ln, scale=math.exp(0.2), bias=shift[:]
-            )
+            for cols in parts(False):
+                nc.scalar.activation(
+                    out=soft[:, t, cols], in_=capped[:, t, cols], func=ACT.Ln, scale=math.exp(0.2), bias=shift[:]
+                )
 
         squared = sb("squared", [P, PACK, S], F32, tag="before_tanh")
         log_den = sb("log_den", [P, PACK, S], F32)
         itf = [sb("itf%d" % t, [P, S], F32) for t in range(PACK)]
         fetched = [sb("fetched%d" % t, [P, S], F32) for t in range(1, PACK)]
         for t in range(PACK):
-            nc.vector.scalar_tensor_tensor(
-                out=dec2[t][:, :S], in0=di[t][:], scalar=0.2, in1=soft[:, t, :], op0=ALU.add, op1=ALU.max
-            )
+            for cols in parts(False):
+                nc.vector.scalar_tensor_tensor(
+                    out=dec2[t][:, cols],
+                    in0=di[t][:, cols],
+                    scalar=0.2,
+                    in1=soft[:, t, cols],
+                    op0=ALU.add,
+                    op1=ALU.max,
+                )
             if t == 1:
-                nc.vector.tensor_tensor(itf[0][:], dec2[0][:].indirect(offsets[:]), intf_sb[:, 0, :], ALU.mult)
+                nc.vector.tensor_tensor(itf[0][:], dec2[0][:].indirect(offsets[:]), intf_first[:, 0, :], ALU.mult)
             if t > 0:
                 nc.scalar.activation(out=fetched[t - 1][:], in_=dec2[t][:].indirect(offsets[:]), func=ACT.Copy)
         total = [sb("total%d" % t, [P, S], F32) for t in range(PACK)]
         aged = [sb("aged%d" % t, [P, S], F32) for t in range(PACK)]
-        for step in range(1, PACK + 2):
-            if step < PACK:
-                nc.vector.tensor_tensor(itf[step][:], fetched[step - 1][:], intf_sb[:, step, :], ALU.mult)
-            if step >= 2:
-                t = step - 2
-                nc.vector.tensor_tensor(aged[t][:], total[t][:], age_sb[:, t, :], ALU.mult)
-                nc.scalar.activation(out=squared[:, t, :], in_=aged[t][:], func=ACT.Square, scale=0.3, bias=one[:])
-                nc.scalar.activation(out=log_den[:, t, :], in_=squared[:, t, :], func=ACT.Ln)
-            if step <= PACK:
-                t = step - 1
-                nc.vector.tensor_tensor(total[t][:], itf[t][:], dec2[t][:, :S], ALU.add)
+        last = PACK - 1
 
-        w2_last = sb("w2_last", [P, 2, 2, P, PACK], BF16, tag="age_sb")
-        w2_tiles = []
-        for h in range(2):
-            deal_into(w2_last[:, h], w2_raw[1], 2 * h, 2, 0, "vector")
-            w2_tiles.extend(quantize_dealt("w2p1_%d" % h, w2_last[:, h], 2))
-        first_product(qi, w2_tiles, 1)
+        def interfere(t):
+            for cols in parts(t == last):
+                nc.vector.tensor_tensor(itf[t][:, cols], fetched[t - 1][:, cols], intf_rest[:, t - 1, cols], ALU.mult)
+
+        def add_own(t):
+            for cols in parts(t == last):
+                nc.vector.tensor_tensor(total[t][:, cols], itf[t][:, cols], dec2[t][:, cols], ALU.add)
+
+        def log_of_den(t):
+            for cols in parts(t == last):
+                nc.vector.tensor_tensor(aged[t][:, cols], total[t][:, cols], age_sb[:, t, cols], ALU.mult)
+            for cols in parts(t == last):
+                nc.scalar.activation(
+                    out=squared[:, t, cols], in_=aged[t][:, cols], func=ACT.Square, scale=0.3, bias=one[:]
+                )
+            for cols in parts(t == last):
+                nc.scalar.activation(out=log_den[:, t, cols], in_=squared[:, t, cols], func=ACT.Ln)
+
+        for t in range(PACK):
+            add_own(t)
+            if t < last - 1:
+                interfere(t + 1)
+            log_of_den(t)
+            if t == last - 1:
+                interfere(t + 1)
+
+        late = sb("late", [P, 2 * P + N, PACK], BF16, tag="age_sb")
+        w2_late = late[:, : 2 * P, :].rearrange("p (t m) j -> p t m j", t=2)
+        deal_into(w2_late, w2_raw[1], 2, 2, 0, "vector")
+        w3_grouped = late[:, 2 * P :, :]
+        nc.vector.tensor_copy(
+            out=w3_grouped.rearrange("p (c i) j -> p c j i", i=4),
+            in_=w3_raw[:].rearrange("p j (c i) -> p c j i", i=4),
+        )
+        first_product(qi[2:], quantize_dealt("w2p1b", w2_late, 2), 1)
+        w3_codes, w3_scales = quantize("w3", w3_grouped.rearrange("p c j -> p (c j)"), N)
+        unit_off = sb("unit_off", [P, PACK], F32)
+        nc.vector.tensor_scalar(unit_off[:], unit_sb[:], -0.4, None, ALU.mult)
 
         bent = sb("bent", [P, PACK, S], F32, tag="before_tanh")
         hid = sb("hid", [P, PACK, S], F32)
         log_rate = [sb("log_rate%d" % t, [P, S], F32) for t in range(PACK)]
 
         def log_of_rate(t):
-            nc.scalar.activation(out=bent[:, t, :], in_=qi[t][:], func=ACT.Tanh)
-            nc.vector.scalar_tensor_tensor(
-                out=log_rate[t][:], in0=bent[:, t, :], scalar=0.9, in1=log_den[:, t, :], op0=ALU.mult, op1=ALU.subtract
-            )
+            for cols in parts(False):
+                nc.scalar.activation(out=bent[:, t, cols], in_=qi[t][:, cols], func=ACT.Tanh)
+                nc.vector.scalar_tensor_tensor(
+                    out=log_rate[t][:, cols],
+                    in0=bent[:, t, cols],
+                    scalar=0.9,
+                    in1=log_den[:, t, cols],
+                    op0=ALU.mult,
+                    op1=ALU.subtract,
+                )
 
         rate = [sb("rate%d" % t, [P, S], F32) for t in range(PACK)]
-        own = [sb("own%d" % t, [P, S], F32) for t in range(PACK)]
+        own = [sb("own%d" % t, [P, S], F32) for t in range(PACK - 1)]
+        last = PACK - 1
 
         def rate_taken(t):
             nc.scalar.activation(out=rate[t][:], in_=log_rate[t][:], func=ACT.Exp)
-            if t < PACK - 1:
-                nc.vector.tensor_scalar(taken[t][:, :S], rate[t][:], unit_off[:, t : t + 1], None, ALU.mult)
-            else:
-                nc.scalar.activation(out=taken[t][:, :S], in_=rate[t][:], func=ACT.Copy, scale=unit_off[:, t : t + 1])
+            nc.vector.tensor_scalar(taken[t][:, :S], rate[t][:], unit_off[:, t : t + 1], None, ALU.mult)
 
-        def hidden(t, parts):
+        def hidden(t):
             nc.scalar.activation(out=own[t][:], in_=rate[t][:], func=ACT.Copy, scale=unit_sb[:, t : t + 1])
-            width = S // parts
-            for h in range(parts):
-                cols = slice(h * width, (h + 1) * width)
-                nc.vector.tensor_tensor(
-                    hid[:, t, cols],
-                    taken[t][:].indirect(offsets[:, h * width // 16 : (h + 1) * width // 16]),
-                    own[t][:, cols],
-                    ALU.add,
-                )
+            nc.vector.tensor_tensor(hid[:, t, :], taken[t][:].indirect(offsets[:]), own[t][:], ALU.add)
 
         for t in range(PACK):
             log_of_rate(t)
         rate_taken(0)
-        hidden(0, 1)
+        hidden(0)
         rate_taken(1)
         rate_taken(2)
-        hidden(1, 1)
-        hidden(2, 1)
-        rate_taken(3)
-        hidden(3, 2)
+        hidden(1)
+        nc.scalar.activation(out=rate[last][:], in_=log_rate[last][:], func=ACT.Exp)
+        hidden(2)
+        own_last = sb("own_last", [P, S], F32)
+        nc.scalar.activation(out=own_last[:], in_=rate[last][:], func=ACT.Copy, scale=unit_sb[:, last : last + 1])
+        other_last = sb("other_last", [P, S], F32)
+        for cols in parts(True):
+            nc.scalar.activation(
+                out=other_last[:, cols],
+                in_=own_last[:].indirect(offsets[:, cols.start // 16 : cols.stop // 16]),
+                func=ACT.Copy,
+            )
+            nc.vector.scalar_tensor_tensor(
+                out=hid[:, last, cols],
+                in0=other_last[:, cols],
+                scalar=-0.4,
+                in1=own_last[:, cols],
+                op0=ALU.mult,
+                op1=ALU.add,
+            )
 
         hid_grouped = []
         for h, engine in enumerate(("scalar", "vector")):

import math
from contextlib import ExitStack

import concourse.mybir as mybir

K, T, S, N, H = 1024, 2048, 512, 128, 512
FLOPS = 2 * (2 * K * H * S + H * N * S)

F32 = mybir.dt.float32
BF16 = mybir.dt.bfloat16
I32 = mybir.dt.int32
U32 = mybir.dt.uint32
U16 = mybir.dt.uint16
U8 = mybir.dt.uint8
FP8X4 = mybir.dt.float8_e4m3fn_x4
ALU = mybir.AluOpType
ACT = mybir.ActivationFunctionType

P = 128
PACK = 4
K_PASS = P * PACK
PASSES = K // K_PASS
SPARE = 16
HALF = S // 2
EXP_CAP = 30.0


def tile_picked_yarpsd_hyp_p_kernel(
    tc, x_words, x_scales, w1, w2, intf, age, unit, w3, offs, off, out
):
    nc = tc.nc
    with ExitStack() as ctx:
        keep = ctx.enter_context(tc.tile_pool(name="keep", bufs=1))
        psum = ctx.enter_context(tc.psum_pool(name="psum", bufs=1))

        def sb(name, shape, dtype, tag=None):
            return keep.tile(shape, dtype, name=name, tag=tag or name, align_bytes=64)

        x_table = [sb("x_table%d" % o, [P, T], U32) for o in range(PASSES)]
        scale_table = sb("scale_table", [P, T], U8)
        picks = keep.tile([P, S // 16], U16, name="picks")
        offsets = keep.tile([P, S // 16], U16, name="offsets")
        nc.vector.memset(scale_table[:].bitcast(I32), 0)

        def load_x(o):
            nc.sync.dma_start(
                out=x_table[o][:].bitcast(I32),
                in_=x_words[o].rearrange("p n t -> p (n t)").bitcast(I32),
            )

        def load_rows(name, src, o):
            raw = sb(name, [P, PACK, src.shape[1]], F32)
            nc.sync.dma_start(
                out=raw[:], in_=src[o * K_PASS : (o + 1) * K_PASS, :].rearrange("(p j) c -> p j c", j=PACK)
            )
            return raw

        for q in range(4):
            nc.sync.dma_start(
                out=scale_table[32 * q : 32 * q + 4 * PASSES, :].bitcast(I32),
                in_=x_scales[:, 4 * q : 4 * q + 4, :].bitcast(I32),
            )
        load_x(0)
        nc.sync.dma_start(out=picks[:], in_=offs)
        w1_raw = [load_rows("w1_raw0", w1, 0)]
        load_x(1)
        w1_raw.append(load_rows("w1_raw1", w1, 1))
        w2_raw = [load_rows("w2_raw0", w2, 0)]
        nc.sync.dma_start(out=offsets[:], in_=off)
        intf_rows = intf.rearrange("(p t) c -> p t c", t=PACK)
        intf_first = sb("intf_first", [P, 1, S], F32)
        nc.sync.dma_start(out=intf_first[:], in_=intf_rows[:, :1, :])
        w2_raw.append(load_rows("w2_raw1", w2, 1))
        intf_rest = sb("intf_rest", [P, PACK - 1, S], F32)
        nc.sync.dma_start(out=intf_rest[:], in_=intf_rows[:, 1:, :])
        age_sb = load_rows("age_sb", age, 0)
        w3_raw = load_rows("w3_raw", w3, 0)
        unit_sb = sb("unit_sb", [P, PACK], F32)
        nc.sync.dma_start(out=unit_sb[:], in_=unit.rearrange("(p t) o -> p (t o)", t=PACK))

        one = sb("one", [P, 1], F32)
        shift = sb("shift", [P, 1], F32)
        nc.vector.memset(one[:], 1.0)
        nc.vector.tensor_scalar(shift[:], one[:], math.exp(0.2), None, ALU.mult)
        dec2 = [sb("dec2_%d" % t, [P, S + SPARE], F32) for t in range(PACK)]
        taken = [sb("taken%d" % t, [P, S + SPARE], F32) for t in range(PACK - 1)]
        for window in dec2 + taken:
            nc.vector.memset(window[:, S:], 0.0)

        x_codes = [sb("x_codes%d" % o, [P, S], U32) for o in range(PASSES)]
        x_bytes = sb("x_bytes", [P, S], U8)
        nc.vector.tensor_copy(x_codes[0][:], x_table[0][:].indirect(picks[:]))
        nc.vector.tensor_copy(x_bytes[:], scale_table[:].indirect(picks[:]))


        def parts(split):
            return [slice(0, HALF), slice(HALF, S)] if split else [slice(0, S)]

        def cast(engine, dst, src):
            if engine == "scalar":
                nc.scalar.activation(out=dst, in_=src, func=ACT.Copy)
            else:
                nc.vector.tensor_copy(out=dst, in_=src)

        def deal_into(grouped, raw, t0, count, m0, engine):
            src = raw[:].rearrange("p j (m t) -> p m j t", t=PACK)[:, :, :, t0 : t0 + count]
            cast(engine, grouped.rearrange("p t m j -> p m j t")[:, m0 : m0 + src.shape[1]], src)

        def deal(name, raw, t0, count, engine):
            grouped = sb(name, [P, count, P, PACK], BF16)
            deal_into(grouped[:], raw, t0, count, 0, engine)
            return grouped[:]

        def quantize(name, flat, words):
            codes = sb(name + "_codes", [P, words], U32)
            scales = sb(name + "_scales", [P, words], U8)
            nc.vector.quantize_mx(out=codes[:].bitcast(FP8X4), scales=scales[:], in_=flat)
            return codes, scales

        def quantize_dealt(name, grouped, count):
            codes, scales = quantize(name, grouped.rearrange("p t m j -> p (t m j)"), count * P)
            return [(codes[:, i * P : (i + 1) * P], scales[:, i * P : (i + 1) * P]) for i in range(count)]

        def first_product(banks, weights, o):
            for t in range(len(banks)):
                nc.tensor.matmul_mx(
                    out=banks[t][:],
                    lhsT=weights[t][0].bitcast(FP8X4),
                    lhsT_scale=weights[t][1],
                    rhs=x_codes[o][:].bitcast(FP8X4),
                    rhs_scale=x_bytes[4 * o :, :],
                    start=(o == 0),
                    stop=(o == PASSES - 1),
                )

        di = [psum.tile([P, S], F32, name="di%d" % t) for t in range(PACK)]
        qi = [psum.tile([P, S], F32, name="qi%d" % t) for t in range(PACK)]

        low = deal("w1g0a", w1_raw[0], 0, 2, "vector")
        high = deal("w1g0b", w1_raw[0], 2, 2, "scalar")
        first_product(di, quantize_dealt("w1p0a", low, 2) + quantize_dealt("w1p0b", high, 2), 0)
        nc.vector.tensor_copy(x_codes[1][:], x_table[1][:].indirect(picks[:]))
        low = deal("w1g1a", w1_raw[1], 0, 2, "vector")
        high = deal("w1g1b", w1_raw[1], 2, 2, "scalar")
        first_product(di, quantize_dealt("w1p1a", low, 2) + quantize_dealt("w1p1b", high, 2), 1)

        grown = sb("grown", [P, PACK, S], F32)
        for t in range(PACK):
            nc.scalar.activation(out=grown[:, t, :], in_=di[t][:], func=ACT.Exp)
        capped = sb("capped", [P, PACK, S], F32)
        nc.vector.tensor_scalar(capped[:], grown[:], math.exp(EXP_CAP), None, ALU.min)

        first_product(qi, quantize_dealt("w2p0", deal("w2g0", w2_raw[0], 0, 4, "vector"), 4), 0)

        w2_early = sb("w2_early", [P, 2, P, PACK], BF16, tag="grown")
        deal_into(w2_early[:], w2_raw[1], 0, 2, 0, "vector")
        first_product(qi[:2], quantize_dealt("w2p1a", w2_early[:], 2), 1)

        soft = sb("soft", [P, PACK, S], F32)
        for t in range(PACK):
            for cols in parts(False):
                nc.scalar.activation(
                    out=soft[:, t, cols], in_=capped[:, t, cols], func=ACT.Ln, scale=math.exp(0.2), bias=shift[:]
                )

        squared = sb("squared", [P, PACK, S], F32, tag="before_tanh")
        log_den = sb("log_den", [P, PACK, S], F32)
        itf = [sb("itf%d" % t, [P, S], F32) for t in range(PACK)]
        fetched = [sb("fetched%d" % t, [P, S], F32) for t in range(1, PACK)]
        for t in range(PACK):
            for cols in parts(False):
                nc.vector.scalar_tensor_tensor(
                    out=dec2[t][:, cols],
                    in0=di[t][:, cols],
                    scalar=0.2,
                    in1=soft[:, t, cols],
                    op0=ALU.add,
                    op1=ALU.max,
                )
            if t == 1:
                nc.vector.tensor_tensor(itf[0][:], dec2[0][:].indirect(offsets[:]), intf_first[:, 0, :], ALU.mult)
            if t > 0:
                nc.scalar.activation(out=fetched[t - 1][:], in_=dec2[t][:].indirect(offsets[:]), func=ACT.Copy)
        total = [sb("total%d" % t, [P, S], F32) for t in range(PACK)]
        aged = [sb("aged%d" % t, [P, S], F32) for t in range(PACK)]
        last = PACK - 1

        def interfere(t):
            for cols in parts(t == last):
                nc.vector.tensor_tensor(itf[t][:, cols], fetched[t - 1][:, cols], intf_rest[:, t - 1, cols], ALU.mult)

        def add_own(t):
            for cols in parts(t == last):
                nc.vector.tensor_tensor(total[t][:, cols], itf[t][:, cols], dec2[t][:, cols], ALU.add)

        def log_of_den(t):
            for cols in parts(t == last):
                nc.vector.tensor_tensor(aged[t][:, cols], total[t][:, cols], age_sb[:, t, cols], ALU.mult)
            for cols in parts(t == last):
                nc.scalar.activation(
                    out=squared[:, t, cols], in_=aged[t][:, cols], func=ACT.Square, scale=0.3, bias=one[:]
                )
            for cols in parts(t == last):
                nc.scalar.activation(out=log_den[:, t, cols], in_=squared[:, t, cols], func=ACT.Ln)

        for t in range(PACK):
            add_own(t)
            if t < last - 1:
                interfere(t + 1)
            log_of_den(t)
            if t == last - 1:
                interfere(t + 1)

        late = sb("late", [P, 2 * P + N, PACK], BF16, tag="age_sb")
        w2_late = late[:, : 2 * P, :].rearrange("p (t m) j -> p t m j", t=2)
        deal_into(w2_late, w2_raw[1], 2, 2, 0, "vector")
        w3_grouped = late[:, 2 * P :, :]
        nc.vector.tensor_copy(
            out=w3_grouped.rearrange("p (c i) j -> p c j i", i=4),
            in_=w3_raw[:].rearrange("p j (c i) -> p c j i", i=4),
        )
        first_product(qi[2:], quantize_dealt("w2p1b", w2_late, 2), 1)
        w3_codes, w3_scales = quantize("w3", w3_grouped.rearrange("p c j -> p (c j)"), N)
        unit_off = sb("unit_off", [P, PACK], F32)
        nc.vector.tensor_scalar(unit_off[:], unit_sb[:], -0.4, None, ALU.mult)

        bent = sb("bent", [P, PACK, S], F32, tag="before_tanh")
        hid = sb("hid", [P, PACK, S], F32)
        log_rate = [sb("log_rate%d" % t, [P, S], F32) for t in range(PACK)]

        def log_of_rate(t):
            for cols in parts(False):
                nc.scalar.activation(out=bent[:, t, cols], in_=qi[t][:, cols], func=ACT.Tanh)
                nc.vector.scalar_tensor_tensor(
                    out=log_rate[t][:, cols],
                    in0=bent[:, t, cols],
                    scalar=0.9,
                    in1=log_den[:, t, cols],
                    op0=ALU.mult,
                    op1=ALU.subtract,
                )

        rate = [sb("rate%d" % t, [P, S], F32) for t in range(PACK)]
        own = [sb("own%d" % t, [P, S], F32) for t in range(PACK - 1)]
        last = PACK - 1

        def rate_taken(t):
            nc.scalar.activation(out=rate[t][:], in_=log_rate[t][:], func=ACT.Exp)
            nc.vector.tensor_scalar(taken[t][:, :S], rate[t][:], unit_off[:, t : t + 1], None, ALU.mult)

        def hidden(t):
            nc.scalar.activation(out=own[t][:], in_=rate[t][:], func=ACT.Copy, scale=unit_sb[:, t : t + 1])
            nc.vector.tensor_tensor(hid[:, t, :], taken[t][:].indirect(offsets[:]), own[t][:], ALU.add)

        for t in range(PACK):
            log_of_rate(t)
        rate_taken(0)
        hidden(0)
        rate_taken(1)
        rate_taken(2)
        hidden(1)
        nc.scalar.activation(out=rate[last][:], in_=log_rate[last][:], func=ACT.Exp)
        hidden(2)
        own_last = sb("own_last", [P, S], F32)
        nc.scalar.activation(out=own_last[:], in_=rate[last][:], func=ACT.Copy, scale=unit_sb[:, last : last + 1])
        other_last = sb("other_last", [P, S], F32)
        for cols in parts(True):
            nc.scalar.activation(
                out=other_last[:, cols],
                in_=own_last[:].indirect(offsets[:, cols.start // 16 : cols.stop // 16]),
                func=ACT.Copy,
            )
            nc.vector.scalar_tensor_tensor(
                out=hid[:, last, cols],
                in0=other_last[:, cols],
                scalar=-0.4,
                in1=own_last[:, cols],
                op0=ALU.mult,
                op1=ALU.add,
            )

        hid_grouped = []
        for h, engine in enumerate(("scalar", "vector")):
            grouped = sb("hid_grouped%d" % h, [P, HALF, PACK], BF16)
            cast(
                engine,
                grouped[:].rearrange("p (c i) t -> p c t i", i=4),
                hid[:, :, h * HALF : (h + 1) * HALF].rearrange("p t (c i) -> p c t i", i=4),
            )
            hid_grouped.append(grouped)
        for h in range(2):
            codes, scales = quantize("hid%d" % h, hid_grouped[h][:].rearrange("p c t -> p (c t)"), HALF)
            acc = psum.tile([P, HALF], F32, name="acc%d" % h, tag="di%d" % h)
            nc.tensor.matmul_mx(
                out=acc[:],
                lhsT=w3_codes[:].bitcast(FP8X4),
                lhsT_scale=w3_scales[:],
                rhs=codes[:].bitcast(FP8X4),
                rhs_scale=scales[:],
                start=True,
                stop=True,
            )
            result = sb("result%d" % h, [P, HALF], F32)
            cast("vector" if h else "scalar", result[:], acc[:])
            nc.sync.dma_start(out=out[:, h * HALF : (h + 1) * HALF], in_=result[:])
